import numpy as np, ml_dtypes
CORES = [2,3,6,7,58,59,62,63,114,115,118,119]
N = 12
import mx_ref
NC = 128
CNT = [[0,16,0,10,2,0,0,58,14,6,18,4],[20,0,38,0,14,14,10,10,10,0,0,12],[6,20,0,46,0,0,0,10,22,10,0,14],[32,2,18,0,26,0,0,10,0,16,6,18],[4,0,8,2,0,24,46,16,0,10,18,0],[0,56,0,6,14,0,10,14,0,0,12,16],[10,0,14,22,42,4,0,0,2,6,28,0],[10,0,10,14,14,44,16,0,10,0,0,10],[0,10,0,4,2,22,10,0,0,34,46,0],[26,0,10,14,8,10,12,4,10,0,0,34],[0,10,30,0,0,8,0,0,14,46,0,20],[20,14,0,10,6,2,24,6,46,0,0,0]]
OFF = [[sum(c[:e]) for e in range(N + 1)] for c in CNT]
BF = ml_dtypes.bfloat16
def setup_inputs(rng):
    def f(*shape):
        return mx_ref.flush((rng.standard_normal(shape, dtype=np.float32) * np.exp2(rng.integers(-2, 3, shape[:-1] + (1,)))).astype(BF))
    return {"w": f(N, 128, 512), "x": f(N, 128, 4 * NC)}
def setup_inputs_blocks(rng):
    d = setup_inputs(rng)
    for k in ("w", "x"): d[k] = mx_ref.spread(d[k], rng, 4)
    return d
def setup_inputs_wide(rng):
    d = setup_inputs(rng)
    for k in ("w", "x"): d[k] = mx_ref.flush((d[k].astype(np.float32) * np.exp2(rng.integers(-8, 9, (N, 1, 1))).astype(np.float32)).astype(BF))
    return d
def setup_inputs_zeros(rng):
    d = setup_inputs(rng); v = d["x"].reshape(N, 128, -1, 4).copy()
    v[np.broadcast_to((rng.random((N, 1, v.shape[2], 1)) < 0.33), v.shape)] = 0
    d["x"] = v.reshape(d["x"].shape)
    return d
def reference(w, x):
    y = np.zeros((N, 128, NC), np.float32)
    for e in range(N):
        t = np.concatenate([x[j][:, 4 * OFF[j][e]:4 * OFF[j][e + 1]] for j in range(N)], axis=1)
        y[e] = mx_ref.matmul(mx_ref.quantize(w[e]), mx_ref.quantize(t))
    return {"y": y}

from concourse.bass import DstId, RemoteDMATransfer
from concourse.mybir import dt, ActivationFunctionType

NC = 128
PAD = 112
GW = 512

SCRATCH = {
    "xt": ("sbuf", [128, 4 * NC], "bfloat16"),
    "wt": ("sbuf", [128, 4 * NC], "bfloat16"),
    "ql": ("sbuf", [128, PAD + NC + PAD], "float8_e4m3fn_x4"),
    "qs": ("sbuf", [128, PAD + NC + PAD], "uint8"),
    "wq": ("sbuf", [128, NC], "float8_e4m3fn_x4"),
    "ws": ("sbuf", [128, NC], "uint8"),
    "bq": ("sbuf", [128, GW], "float8_e4m3fn_x4"),
    "bs": ("sbuf", [128, GW], "uint8"),
    "ps": ("psum", [128, 3 * 512], "float32"),
    "yt": ("sbuf", [128, NC], "float32"),
}
SEMAPHORES = ["xl", "wl", "qx", "qw", "c1", "s1", "lt", "snt", "me", "m1", "m2", "cp", "st"]


def _bits(mask):
    return [b for b in range(mask.bit_length()) if (mask >> b) & 1]


def _mask(bits):
    return sum(1 << b for b in bits)


def _plan(T, topo):
    cores = list(T.cores)
    cnt = T.tables["CNT"]
    n = len(cores)
    off = [[sum(row[:e]) for e in range(n + 1)] for row in cnt]
    chips = []
    for c in cores:
        if topo.chip(c) not in chips:
            chips.append(topo.chip(c))
    mem = [[r for r in range(n) if topo.chip(cores[r]) == ch] for ch in chips]
    grp = [chips.index(topo.chip(c)) for c in cores]
    lane = []
    for r in range(n):
        d = topo.die(cores[r])
        same = [q for q in mem[grp[r]] if topo.die(cores[q]) == d]
        lane.append((d, same.index(r)))
    relay = {}
    for r in range(n):
        relay[(grp[r], lane[r])] = r

    def run(j, x):
        return off[j][mem[x][0]], off[j][mem[x][-1] + 1]

    info = []
    for r in range(n):
        x = grp[r]
        wins = [j for j in range(n) if grp[j] != x and lane[j] == lane[r] and run(j, x)[1] > run(j, x)[0]]
        width = sum(run(j, x)[1] - run(j, x)[0] for j in wins)
        a, b = run(r, x)
        if a <= NC - b:
            lbase = PAD - width
            tile = (PAD, PAD + b)
            blk = (lbase, PAD + b)
        else:
            lbase = PAD + NC
            tile = (PAD + a, PAD + NC)
            blk = (PAD + a, lbase + width)
        wb = {}
        p = lbase
        for j in wins:
            wb[j] = p
            p += run(j, x)[1] - run(j, x)[0]
        info.append({"wins": wins, "l": width, "lbase": lbase, "tile": tile, "blk": blk, "wb": wb})
    return {"cores": cores, "cnt": cnt, "n": n, "off": off, "mem": mem, "grp": grp, "lane": lane, "relay": relay,
            "run": run, "info": info}


def _view(lo, hi, top):
    if hi - lo < NC:
        hi = min(top, lo + NC)
        lo = hi - NC
    return lo, hi


def rank_program(g, core, T, topo):
    me = T.rank_of(core)
    if me is None:
        return
    S = T.sem
    pl = _plan(T, topo)
    cores, cnt, n, off, mem, grp, lane, relay, run, info = (pl[k] for k in (
        "cores", "cnt", "n", "off", "mem", "grp", "lane", "relay", "run", "info"))
    x = grp[me]
    mine = info[me]
    peers = [p for p in mem[x] if p != me]
    u8 = dt.uint8

    def gbase(r):
        base, p = {}, 0
        for q in mem[grp[r]]:
            if q != r:
                base[q] = p
                p += info[q]["blk"][1] - info[q]["blk"][0]
        return base, p

    g.sync.dma_start(T.xt[:], T.x[:]).then_inc(S.xl, 16)
    g.sync.dma_start(T.wt[:], T.w[:]).then_inc(S.wl, 16)
    g.vector.wait_ge(S.xl, 16)
    g.vector.quantize_mx(T.ql[:, PAD:PAD + NC], T.qs[:, PAD:PAD + NC], T.xt[:]).then_inc(S.qx, 1)
    g.vector.wait_ge(S.wl, 16)
    g.vector.quantize_mx(T.wq[:], T.ws[:], T.wt[:]).then_inc(S.qw, 1)

    far = [y for y in range(len(mem)) if y != x and run(me, y)[1] > run(me, y)[0]]
    far.sort(key=lambda y: run(me, y)[1] - run(me, y)[0])
    on_mask = topo.mask(core, cores[peers[0]])
    off_mask = on_mask
    for y in far:
        off_mask &= topo.mask(core, cores[relay[(y, lane[me])]])
    share = 1
    while share * 2 * len(far) <= len(_bits(off_mask)):
        share *= 2
    far_mask = {y: _mask(_bits(off_mask)[i * share:(i + 1) * share]) for i, y in enumerate(far)}
    home_mask = on_mask & ~off_mask
    n_home, n_on = len(_bits(home_mask)), len(_bits(on_mask))
    sent = 0

    def ids(rs):
        return [DstId(rid=topo.addr(cores[r])[0], pnc=topo.addr(cores[r])[1]) for r in rs]

    def out_of_chip(buf, sem, cast):
        k = 0
        for y in far:
            r = relay[(y, lane[me])]
            a, b = run(me, y)
            d = info[r]["wb"][me]
            src, dst = buf[:, PAD + a:PAD + b], buf[:, d:d + b - a]
            if cast:
                src, dst = src.bitcast(u8), dst.bitcast(u8)
            rid, pid, _ = topo.addr(cores[r])
            g.remote_dma(dst, src, sem, S.snt, pid, rid, far_mask[y])
            k += share
        return k

    def to_peers(src_buf, dst_buf, lo, hi, mask, cast):
        src = src_buf[:, lo:hi]
        dsts = []
        for p in peers:
            d = gbase(p)[0][me] + lo - mine["blk"][0]
            dsts.append(dst_buf[:, d:d + hi - lo])
        if cast:
            src, dsts = src.bitcast(u8), [d.bitcast(u8) for d in dsts]
        g.remote_dma_fused([RemoteDMATransfer(dst_ids=ids(peers), dma_engine_mask=mask, remote_sem=S.lt,
                                              srcs=[src], dsts=dsts)], local_sem=S.snt)
        return len(_bits(mask))

    g.wait_ge(S.qx, 1)
    sent += out_of_chip(T.ql, S.c1, True)
    sent += to_peers(T.ql, T.bq, mine["tile"][0], mine["tile"][1], home_mask, True)
    sent += out_of_chip(T.qs, S.s1, False)
    landed = share * len(mine["wins"])
    lz = (mine["lbase"], mine["lbase"] + mine["l"])
    g.wait_ge(S.c1, landed)
    sent += to_peers(T.ql, T.bq, lz[0], lz[1], on_mask, True)
    g.wait_ge(S.s1, landed)
    sent += to_peers(T.qs, T.bs, mine["blk"][0], mine["blk"][1], on_mask, False)
    g.wait_ge(S.snt, sent)

    base, top = gbase(me)
    early, late = [], []
    for j in range(n):
        c = cnt[j][me]
        if c == 0:
            continue
        ycol = sum(cnt[i][me] for i in range(j))
        if grp[j] == x:
            late.append((base[j] + PAD + off[j][me] - info[j]["blk"][0], ycol, c))
        else:
            q = relay[(x, lane[j])]
            col = info[q]["wb"][j] + off[j][me] - run(j, x)[0]
            if q == me:
                early.append((col, ycol, c))
            else:
                late.append((base[q] + col - info[q]["blk"][0], ycol, c))
    late.sort()

    def span(runs):
        return _view(runs[0][0], runs[-1][0] + runs[-1][2], top)

    def copies(runs):
        return sum(max(64, r[2]) for r in runs)

    best = None
    for h in range(1, len(late) + 1):
        a, b = late[:h], late[h:]
        va = span(a)
        t1 = va[1] - va[0] + 16
        t = t1 + copies(a)
        if va[1] - va[0] > 512:
            continue
        if b:
            vb = span(b)
            if vb[1] - vb[0] > 512:
                continue
            t = max(t, t1 + vb[1] - vb[0] + 16 + copies(b))
        if best is None or t < best[0]:
            best = (t, h)
    h = best[1]
    parts = [late[:h], late[h:]]

    g.tensor.wait_ge(S.qw, 1)
    done = 0
    if early:
        if mine["lbase"] < PAD:
            ev = (lz[0], lz[0] + max(NC, mine["l"]))
        else:
            ev = (lz[1] - max(NC, mine["l"]), lz[1])
        g.tensor.wait_ge(S.qx, 1)
        g.tensor.wait_ge(S.c1, landed)
        g.tensor.wait_ge(S.s1, landed)
        g.tensor.matmul_mx(T.ps[:, 0:ev[1] - ev[0]], T.wq[:], T.ws[:], T.ql[:, ev[0]:ev[1]], T.qs[:, ev[0]:ev[1]],
                           True, True).then_inc(S.me, 1)
        g.vector.wait_ge(S.me, 1)
        for col, ycol, c in early:
            g.vector.tensor_copy(T.yt[:, ycol:ycol + c], T.ps[:, col - ev[0]:col - ev[0] + c]).then_inc(S.cp, 1)
            done += 1
    g.tensor.wait_ge(S.lt, len(peers) * (n_home + 2 * n_on))
    for i, (runs, sem) in enumerate(zip(parts, (S.m1, S.m2))):
        if not runs:
            continue
        lo, hi = span(runs)
        bank = 512 * (i + 1)
        g.tensor.matmul_mx(T.ps[:, bank:bank + hi - lo], T.wq[:], T.ws[:], T.bq[:, lo:hi], T.bs[:, lo:hi],
                           True, True).then_inc(sem, 1)
        q = g.vector if i == 0 else g.scalar
        q.wait_ge(sem, 1)
        for col, ycol, c in runs:
            dst, src = T.yt[:, ycol:ycol + c], T.ps[:, bank + col - lo:bank + col - lo + c]
            if i == 0:
                g.vector.tensor_copy(dst, src).then_inc(S.cp, 1)
            else:
                g.scalar.activation(dst, src, ActivationFunctionType.Copy).then_inc(S.cp, 1)
            done += 1

    g.sync.wait_ge(S.cp, done)
    g.sync.dma_start(T.y[:], T.yt[:]).then_inc(S.st, 16)
    g.sync.wait_ge(S.st, 16)
